import numpy as np
import ml_dtypes


def mxq(x, axis, fmt="e4m3"):
    dtype, down = {"e4m3": (ml_dtypes.float8_e4m3fn, 7), "e5m2": (ml_dtypes.float8_e5m2, 14)}[fmt]
    v = np.moveaxis(np.asarray(x, np.float32).astype(ml_dtypes.bfloat16).astype(np.float64), axis, -1)
    blocks = v.reshape(v.shape[:-1] + (-1, 32))
    amax = np.abs(blocks).max(-1, keepdims=True)
    byte = np.maximum(np.where(amax > 0, np.frexp(amax)[1] - 1 + 127, 0) - down, 1)
    scale = np.exp2(byte - 127.0)
    codes = (blocks / scale).astype(np.float32).astype(dtype).astype(np.float64)
    return np.moveaxis((codes * scale).reshape(v.shape), -1, axis)


WIDE = False


def mx_kscale(k):
    if not WIDE:
        return np.ones(k)
    levels = np.array([10, -10, 5, -5, 0])
    if k % 512:
        return np.exp2(np.random.permutation(np.resize(levels, k // 32))).repeat(32)
    a = np.empty((k // 512, 16))
    for p in range(k // 512):
        a[p, :8] = np.random.permutation(np.resize(levels, 8))
        for g in range(8):
            far = levels[np.abs(levels - a[p, g]) >= 10]
            a[p, g + 8] = far[np.random.randint(len(far))]
    return np.exp2(a.ravel()).repeat(32)


BF16 = ml_dtypes.bfloat16


def bf(x):
    return np.asarray(x, np.float32).astype(BF16)


def f64(x):
    return np.asarray(x).astype(np.float64)


E2M1 = np.array([0.0, 0.5, 1.0, 1.5, 2.0, 3.0, 4.0, 6.0, -0.0, -0.5, -1.0, -1.5, -2.0, -3.0, -4.0, -6.0])


def pack_weight(w, fmt):
    k, n = w.shape
    w = f64(bf(w)).reshape(k // 32, 32, n)
    amax = np.abs(w).max(1)
    if fmt == "e4m3":
        byte = np.frexp(amax)[1] - 1 + 127 - 7
    else:
        mant, ex = np.frexp(amax / 6.0)
        byte = np.where(mant > 0.5, ex, ex - 1) + 127
    byte = np.clip(np.where(amax > 0, byte, 1), 1, 254)
    scaled = (w * np.exp2(127.0 - byte)[:, None, :]).reshape(k, n).astype(np.float32)
    by_word = np.ascontiguousarray(scaled.reshape(k // 512, 128, 4, n).transpose(0, 1, 3, 2))
    if fmt == "e4m3":
        words = by_word.astype(ml_dtypes.float8_e4m3fn).view(np.uint8)
    else:
        c = by_word.astype(ml_dtypes.float4_e2m1fn).view(np.uint8) & 0xF
        words = c[..., 0::2] | (c[..., 1::2] << 4)
    return np.ascontiguousarray(words), np.ascontiguousarray(byte.astype(np.uint8).reshape(k // 512, 16, n))


def unpack_weight(words, scales, fmt):
    g, p, n, _ = words.shape
    if fmt == "e4m3":
        vals = np.ascontiguousarray(words).view(ml_dtypes.float8_e4m3fn).astype(np.float64)
    else:
        nib = np.empty((g, p, n, 4), np.uint8)
        nib[..., 0::2] = words & 0xF
        nib[..., 1::2] = words >> 4
        vals = E2M1[nib]
    vals = vals * np.repeat(np.exp2(scales.astype(np.float64) - 127.0), 8, axis=1)[..., None]
    return vals.transpose(0, 1, 3, 2).reshape(g * 512, n)
def pack4(w):
    words, scales = pack_weight(w, "e2m1")
    return words.reshape(words.shape[0], 128, -1), scales


def unpack4(words, scales):
    return unpack_weight(words.reshape(words.shape[0], 128, -1, 2), scales, "e2m1")


def planes(Y):
    n, m = Y.shape
    b = f64(bf(Y)).reshape(n // 32, 32, m)
    amax = np.abs(b).max(1)
    byte = np.clip(np.where(amax > 0, np.frexp(amax)[1] - 1 + 127 - 7, 1), 1, 254)
    codes = (b * np.exp2(127.0 - byte)[:, None, :]).reshape(n, m).astype(np.float32).astype(ml_dtypes.float8_e4m3fn).view(np.uint8)
    words = codes.reshape(n // 512, 128, 4, m).transpose(0, 1, 3, 2)
    return np.ascontiguousarray(words), np.ascontiguousarray(byte.astype(np.uint8).reshape(n // 512, 16, m))


T, D, R, E = 4096, 1024, 512, 256

def softmax_rows(z):
    e = np.exp(z - z.max(axis=1, keepdims=True))
    return e / e.sum(axis=1, keepdims=True)

def setup_inputs():
    rn = np.random.randn
    s = mx_kscale(D)
    t = mx_kscale(T)
    x_words, x_scales = pack_weight(rn(D, T) * s[:, None], "e4m3")
    wr_words, wr_scales = pack4(rn(D, E) / np.sqrt(D) / s[:, None])
    load = np.exp(0.5 * rn(E))
    c = np.exp(0.8 * rn(R))
    return {
        "x_words": x_words, "x_scales": x_scales,
        "wr_words": wr_words, "wr_scales": wr_scales,
        "a": bf(rn(D, R) / np.sqrt(D) / s[:, None]),
        "loads": bf(load / load.mean()),
        "token_weight": bf(np.sqrt(E) * np.exp(0.3 * rn(T)) * t),
        "token_gate": bf(4.0 / np.sqrt(E) * np.exp(0.3 * rn(T)) / t),
        "rank_scale": bf(c),
        "acc": bf(0.3 * c[:, None] * rn(R, E)),
    }

def reference(x_words, x_scales, wr_words, wr_scales, a, loads, token_weight, token_gate, rank_scale, acc):
    X = unpack_weight(x_words, x_scales, "e4m3")
    Wr = unpack4(wr_words, wr_scales)
    f = f64(loads)[None, :]
    S = softmax_rows(X.T @ Wr)
    dZ = S * (f - (S * f).sum(axis=1, keepdims=True)) * f64(token_weight)[:, None]
    H = (X.T @ mxq(f64(a), 0, "e4m3")) * f64(token_gate)[:, None]
    G = mxq(H, 0, "e4m3").T @ mxq(dZ, 0, "e4m3")
    y = G * f64(rank_scale)[:, None] + f64(acc)
    Y = y
    words, scales = planes(Y)
    return y, words, scales

@@ -1,0 +1,346 @@
+from contextlib import ExitStack
+
+import concourse.mybir as mybir
+from concourse.masks import make_identity
+
+T, D, R, E = 4096, 1024, 512, 256
+FLOPS = 2 * T * D * (R + E) + 2 * T * R * E
+
+F32 = mybir.dt.float32
+BF16 = mybir.dt.bfloat16
+I32 = mybir.dt.int32
+U8 = mybir.dt.uint8
+FP8X4 = mybir.dt.float8_e4m3fn_x4
+FP4X4 = mybir.dt.float4_e2m1fn_x4
+ALU = mybir.AluOpType
+ACT = mybir.ActivationFunctionType
+AX = mybir.AxisListType
+
+P = 128
+PACK = 4
+KP = P * PACK
+NG = T // KP
+DG = D // KP
+EARLY = 2
+CV = 128
+CV_LAST = 256
+A_SCALAR = 48
+LOADS_ROW = 16
+
+
+def tile_router_balance_adapter_gradient_k4_kernel(
+    tc, x_words, x_scales, wr_words, wr_scales, a, loads, token_weight, token_gate, rank_scale, acc,
+    out_0, out_1, out_2,
+):
+    nc = tc.nc
+    with ExitStack() as ctx:
+        keep = ctx.enter_context(tc.tile_pool(name="keep", bufs=1))
+        work = ctx.enter_context(tc.tile_pool(name="work", bufs=2))
+        psum = ctx.enter_context(tc.psum_pool(name="psum", bufs=1))
+        ctx.enter_context(tc.manual_schedule())
+
+        chunks = [(0, EARLY), (EARLY, NG)]
+        xs_raw = []
+        xs_perm = []
+        for ci, (g0, g1) in enumerate(chunks):
+            n = g1 - g0
+            xs_raw.append(keep.tile([P, DG, n * KP // 4], I32, name="xs_raw%d" % ci, align_bytes=64))
+            xs_perm.append(keep.tile([P, PACK, DG * n * P // 4], I32, name="xs_perm%d" % ci, align_bytes=64))
+        wr_sb = keep.tile([P, DG, 2 * E], U8, align_bytes=64)
+        wr_sc = keep.tile([P, DG, E], U8, align_bytes=64)
+        small = keep.tile([P, KP], BF16, align_bytes=64)
+        small_p = keep.tile([P, PACK, P], BF16, align_bytes=64)
+        ident = keep.tile([P, P], BF16, align_bytes=64)
+        tok = keep.tile([P, PACK, 2 * NG], F32, align_bytes=64)
+        f_sb = keep.tile([P, E], F32, align_bytes=64)
+        warm = keep.tile([P, 2], F32, align_bytes=64)
+        junk = keep.tile([P, E], F32, align_bytes=64)
+        a_codes = keep.tile([P, DG, R], I32, align_bytes=64)
+        a_sc = keep.tile([P, DG, R], U8, align_bytes=64)
+        acc_sb = keep.tile([P, PACK, E], BF16, align_bytes=64)
+        rs_sb = keep.tile([P, PACK], BF16, align_bytes=64)
+        x_raw = [keep.tile([P, DG, KP], I32, name="x_raw%d" % k, align_bytes=64) for k in range(NG)]
+        a_raw = [keep.tile([P, PACK, R], BF16, name="a_raw%d" % g, align_bytes=64) for g in range(DG)]
+        a_grp = [keep.tile([P, R, PACK], BF16, name="a_grp%d" % g, align_bytes=64) for g in range(DG)]
+        h_codes = [keep.tile([P, R], I32, name="h_codes%d" % k, align_bytes=64) for k in range(NG)]
+        h_sc = [keep.tile([P, R], U8, name="h_sc%d" % k, align_bytes=64) for k in range(NG)]
+        z_codes = [keep.tile([P, E], I32, name="z_codes%d" % k, align_bytes=64) for k in range(NG)]
+        z_sc = [keep.tile([P, E], U8, name="z_sc%d" % k, align_bytes=64) for k in range(NG)]
+
+        xw = x_words.rearrange("g p n t -> p g (n t)")
+        xs = x_scales.rearrange("g (q r) n -> r q g n", r=4)
+        ws = wr_scales.rearrange("g (q r) n -> r q g n", r=4)
+
+        def load_x(k):
+            nc.sync.dma_start(out=x_raw[k][:], in_=xw[:, :, 4 * KP * k : 4 * KP * (k + 1)].bitcast(I32))
+
+        def load_xs(ci):
+            g0, g1 = chunks[ci]
+            for r in range(4):
+                nc.sync.dma_start(out=xs_raw[ci][r:P:32, :, :], in_=xs[r][:, :, KP * g0 : KP * g1].bitcast(I32))
+
+        def load_a(g):
+            nc.sync.dma_start(out=a_raw[g][:], in_=a[KP * g : KP * (g + 1), :].rearrange("(p j) c -> p j c", j=PACK))
+
+        nc.vector.memset(xs_raw[0][:], 0)
+        nc.vector.memset(wr_sc[:].bitcast(I32), 0)
+        nc.vector.memset(small[:], 0.0)
+        nc.vector.memset(warm[:], 0.0)
+        nc.vector.memset(xs_raw[1][:], 0)
+        nc.scalar.activation(out=warm[:, 1:2], in_=warm[:, 0:1], func=ACT.Exp)
+
+        make_identity(nc, ident[:])
+        load_a(0)
+        load_xs(0)
+        load_x(0)
+        load_a(1)
+        nc.sync.dma_start(out=wr_sb[:].bitcast(I32), in_=wr_words.rearrange("g p n -> p g n").bitcast(I32))
+        for r in range(4):
+            nc.sync.dma_start(out=wr_sc[r:P:32, :, :].bitcast(I32), in_=ws[r].bitcast(I32))
+        nc.sync.dma_start(out=small[0:NG, :], in_=token_weight.rearrange("(k n) -> k n", k=NG))
+        nc.sync.dma_start(out=small[NG : 2 * NG, :], in_=token_gate.rearrange("(k n) -> k n", k=NG))
+        nc.sync.dma_start(out=small[LOADS_ROW : LOADS_ROW + 1, 0:E], in_=loads.rearrange("(o n) -> o n", o=1))
+        load_x(1)
+        load_xs(1)
+        for k in range(2, NG):
+            load_x(k)
+        nc.sync.dma_start(out=acc_sb[:], in_=acc.rearrange("(p t) e -> p t e", t=PACK))
+        nc.sync.dma_start(out=rs_sb[:], in_=rank_scale.rearrange("(p t) -> p t", t=PACK))
+
+        xp = {}
+        zb = {}
+        nmax = {}
+        ex = {}
+        s0 = {}
+        gt = {}
+        hb = {}
+        hint = {}
+        dz = {}
+
+        def perm_scales(ci):
+            nc.vector.tensor_copy(
+                out=xs_perm[ci][:].rearrange("p t (c r) -> p t c r", r=2),
+                in_=xs_raw[ci][:].rearrange("p g (c t r) -> p t (g c) r", t=PACK, r=2),
+            )
+
+        def perm_x(k):
+            xp[k] = work.tile([P, PACK, DG * P], I32, name="xp", tag="xp", bufs=3, align_bytes=64)
+            nc.vector.tensor_copy(
+                out=xp[k][:].rearrange("p t (c r) -> p t c r", r=8),
+                in_=x_raw[k][:].rearrange("p g (q t r) -> p t (g q) r", t=PACK, r=8),
+            )
+
+        def x_operand(k, t, g):
+            ci = 0 if k < EARLY else 1
+            g0, g1 = chunks[ci]
+            w0 = (g * (g1 - g0) + k - g0) * (P // 4)
+            return xp[k][:, t, P * g : P * (g + 1)].bitcast(FP8X4), xs_perm[ci][:, t, w0 : w0 + P // 4].bitcast(U8)
+
+        def router(k):
+            zb[k] = []
+            for u in range(2):
+                z = psum.tile([P, 2, E], F32, name="z", tag="z", bufs=3)
+                zb[k].append(z)
+                for tt in range(2):
+                    for h in range(E // P):
+                        for g in range(DG):
+                            codes, scales = x_operand(k, 2 * u + tt, g)
+                            nc.tensor.matmul_mx(
+                                out=z[:, tt, P * h : P * (h + 1)],
+                                lhsT=codes,
+                                lhsT_scale=scales,
+                                rhs=wr_sb[:, g, 2 * P * h : 2 * P * (h + 1)].bitcast(FP4X4),
+                                rhs_scale=wr_sc[:, g, P * h : P * (h + 1)],
+                                start=(g == 0),
+                                stop=(g == DG - 1),
+                            )
+
+        def row_max(k):
+            nmax[k] = work.tile([P, PACK], F32, name="nmax", tag="nmax")
+            for u in range(2):
+                nc.vector.tensor_reduce(
+                    out=nmax[k][:, 2 * u : 2 * u + 2], in_=zb[k][u][:], axis=AX.X, op=ALU.max, negate=True
+                )
+
+        def exps(k):
+            ex[k] = work.tile([P, PACK, E], F32, name="ex", tag="ex", align_bytes=64)
+            s0[k] = work.tile([P, PACK], F32, name="s0", tag="s0")
+            for t in range(PACK):
+                nc.scalar.activation(
+                    out=ex[k][:, t, :], in_=zb[k][t // 2][:, t % 2, :], func=ACT.Exp,
+                    bias=nmax[k][:, t : t + 1], scale=1.0, accum_out=s0[k][:, t : t + 1],
+                )
+
+        def jacobian(k, f_ps):
+            ns1 = work.tile([P, PACK], F32, name="ns1", tag="ns1")
+            rinv = work.tile([P, PACK], F32, name="rinv", tag="rinv")
+            alpha = work.tile([P, PACK], F32, name="alpha", tag="alpha")
+            nmean = work.tile([P, PACK], F32, name="nmean", tag="nmean")
+            gt[k] = work.tile([P, PACK, E], F32, name="gt", tag="gt", align_bytes=64)
+            for t in range(PACK):
+                if t == PACK - 1:
+                    nc.vector.reciprocal(out=rinv[:], in_=s0[k][:])
+                nc.vector.scalar_tensor_tensor(
+                    out=junk[:], in0=ex[k][:, t, :], scalar=-1.0, in1=f_ps[:], op0=ALU.mult, op1=ALU.mult,
+                    accum_out=ns1[:, t : t + 1],
+                )
+            eng = nc.gpsimd if k + 1 < NG else nc.vector
+            eng.tensor_tensor(out=alpha[:], in0=tok[:, :, k], in1=rinv[:], op=ALU.mult)
+            eng.tensor_tensor(out=nmean[:], in0=ns1[:], in1=rinv[:], op=ALU.mult)
+            if k + 1 == NG:
+                quant_dz(k - 1)
+            for t in range(PACK):
+                eng.tensor_scalar(
+                    out=gt[k][:, t, :], in0=f_sb[:], scalar1=nmean[:, t : t + 1], scalar2=alpha[:, t : t + 1],
+                    op0=ALU.add, op1=ALU.mult,
+                )
+
+        def make_dz(k):
+            dz[k] = work.tile([P, E, PACK], BF16, name="dz", tag="dz", align_bytes=64)
+            nc.vector.tensor_tensor(
+                out=dz[k][:].rearrange("p (c i) t -> p c t i", i=4),
+                in0=ex[k][:].rearrange("p t (c i) -> p c t i", i=4),
+                in1=gt[k][:].rearrange("p t (c i) -> p c t i", i=4),
+                op=ALU.mult,
+            )
+
+        def adapter(k):
+            hb[k] = work.tile([P, PACK, R], BF16, name="hb", tag="hb", align_bytes=64)
+            for t in range(PACK):
+                h = psum.tile([P, R], F32, name="h", tag="h", bufs=4)
+                for g in range(DG):
+                    codes, scales = x_operand(k, t, g)
+                    nc.tensor.matmul_mx(
+                        out=h[:], lhsT=codes, lhsT_scale=scales, rhs=a_codes[:, g, :].bitcast(FP8X4),
+                        rhs_scale=a_sc[:, g, :], start=(g == 0), stop=(g == DG - 1),
+                    )
+                nc.scalar.activation(
+                    out=hb[k][:, t, :], in_=h[:], func=ACT.Copy, scale=tok[:, t, NG + k : NG + k + 1]
+                )
+
+        def h_views(k, c0, c1):
+            dst = hint[k][:, c0:c1, :].rearrange("p (c i) t -> p c t i", i=4)
+            src = hb[k][:, :, c0:c1].rearrange("p t (c i) -> p c t i", i=4)
+            return dst, src
+
+        def interleave_h_scalar(k):
+            hint[k] = work.tile([P, R, PACK], BF16, name="hint", tag="hint", align_bytes=64)
+            dst, src = h_views(k, CV if k + 1 < NG else CV_LAST, R)
+            nc.scalar.copy(out=dst, in_=src)
+
+        def interleave_h_vector(k):
+            dst, src = h_views(k, 0, CV if k + 1 < NG else CV_LAST)
+            nc.vector.tensor_copy(out=dst, in_=src)
+
+        def quant_h(k):
+            nc.vector.quantize_mx(
+                out=h_codes[k][:].bitcast(FP8X4), scales=h_sc[k][:], in_=hint[k][:].rearrange("p c t -> p (c t)")
+            )
+
+        def quant_dz(k):
+            nc.vector.quantize_mx(
+                out=z_codes[k][:].bitcast(FP8X4), scales=z_sc[k][:], in_=dz[k][:].rearrange("p c t -> p (c t)")
+            )
+
+        def group_a(g):
+            dst = a_grp[g][:].rearrange("p (t m) j -> p m t j", t=PACK)
+            src = a_raw[g][:].rearrange("p j (m t) -> p m t j", t=PACK)
+            nc.scalar.copy(out=dst[:, :A_SCALAR], in_=src[:, :A_SCALAR])
+            nc.vector.tensor_copy(out=dst[:, A_SCALAR:], in_=src[:, A_SCALAR:])
+
+        def quant_a(g):
+            nc.vector.quantize_mx(
+                out=a_codes[:, g, :].bitcast(FP8X4), scales=a_sc[:, g, :], in_=a_grp[g][:].rearrange("p c j -> p (c j)")
+            )
+
+        def grad_pass(gacc, t, k):
+            nc.tensor.matmul_mx(
+                out=gacc[:], lhsT=h_codes[k][:, P * t : P * (t + 1)].bitcast(FP8X4),
+                lhsT_scale=h_sc[k][:, P * t : P * (t + 1)], rhs=z_codes[k][:].bitcast(FP8X4),
+                rhs_scale=z_sc[k][:], start=(k == 0), stop=(k == NG - 1),
+            )
+
+        group_a(0)
+        perm_scales(0)
+        perm_x(0)
+        quant_a(0)
+        group_a(1)
+        router(0)
+        nc.vector.tensor_copy(
+            out=small_p[:].rearrange("p t (q r) -> p t q r", r=8),
+            in_=small[:].rearrange("p (q t r) -> p t q r", t=PACK, r=8),
+        )
+        quant_a(1)
+        row_max(0)
+        f_ps = psum.tile([P, E], F32, name="f_ps", tag="f")
+        nc.tensor.matmul(
+            f_ps[:], lhsT=ident[:, LOADS_ROW : LOADS_ROW + 1].to_broadcast([P, P]), rhs=small[:, 0:E],
+            start=True, stop=True,
+        )
+        tok_ps = psum.tile([P, PACK, P], BF16, name="tok_ps", tag="h", bufs=4)
+        for t in range(PACK):
+            nc.tensor.transpose(tok_ps[:, t, :], small_p[:, t, :], ident[:])
+        nc.scalar.copy(out=tok[:], in_=tok_ps[:, :, 0 : 2 * NG])
+        nc.scalar.copy(out=f_sb[:], in_=f_ps[:])
+        exps(0)
+        perm_x(1)
+        adapter(0)
+        interleave_h_scalar(0)
+
+        gaccs = []
+        for k in range(NG):
+            jacobian(k, f_ps)
+            if k + 1 < NG:
+                router(k + 1)
+                row_max(k + 1)
+                exps(k + 1)
+            if k == 0:
+                perm_scales(1)
+            if k + 2 < NG:
+                perm_x(k + 2)
+            if k + 1 < NG:
+                interleave_h_vector(k)
+                if k > 0:
+                    quant_dz(k - 1)
+                quant_h(k)
+                make_dz(k)
+                adapter(k + 1)
+                interleave_h_scalar(k + 1)
+            else:
+                for t in range(PACK):
+                    grad_pass(gaccs[t], t, k - 1)
+                make_dz(k)
+                interleave_h_vector(k)
+                quant_dz(k)
+                quant_h(k)
+            if k + 2 == NG:
+                for t in range(PACK):
+                    if t < 3:
+                        gacc = psum.tile([P, E], F32, name="gz", tag="z", bufs=3)
+                    else:
+                        gacc = psum.tile([P, E], F32, name="gh", tag="h", bufs=4)
+                    gaccs.append(gacc)
+                    for kk in range(NG - 2):
+                        grad_pass(gacc, t, kk)
+
+        y = keep.tile([P, PACK, E], F32, align_bytes=64)
+        yb = keep.tile([P, E, PACK], BF16, align_bytes=64)
+        y_codes = keep.tile([P, E], I32, align_bytes=64)
+        y_sc = keep.tile([P, E], U8, align_bytes=64)
+        for t in range(PACK):
+            grad_pass(gaccs[t], t, NG - 1)
+        for t in range(PACK):
+            nc.vector.scalar_tensor_tensor(
+                out=y[:, t, :], in0=gaccs[t][:], scalar=rs_sb[:, t : t + 1], in1=acc_sb[:, t, :],
+                op0=ALU.mult, op1=ALU.add,
+            )
+        nc.sync.dma_start(out=out_0.rearrange("(p t) e -> p t e", t=PACK), in_=y[:])
+        nc.vector.tensor_copy(
+            out=yb[:].rearrange("p (c i) t -> p c t i", i=4), in_=y[:].rearrange("p t (c i) -> p c t i", i=4)
+        )
+        nc.vector.quantize_mx(out=y_codes[:].bitcast(FP8X4), scales=y_sc[:], in_=yb[:].rearrange("p c t -> p (c t)"))
+        nc.sync.dma_start(out=out_1[0].rearrange("p m t -> p (m t)").bitcast(I32), in_=y_codes[:])
+        for q in range(4):
+            nc.sync.dma_start(
+                out=out_2[0][4 * q : 4 * q + 4, :].bitcast(I32), in_=y_sc[32 * q : 32 * q + 4, :].bitcast(I32)
+            )

@@ -22,7 +22,7 @@ KP = P * PACK
 NG = T // KP
 DG = D // KP
 EARLY = 2
-CV = 128
+CV = 32
 CV_LAST = 256
 A_SCALAR = 48
 LOADS_ROW = 16
@@ -155,12 +155,12 @@ def tile_router_balance_adapter_gradient_k4_kernel(
                                 stop=(g == DG - 1),
                             )
 
-        def row_max(k):
-            nmax[k] = work.tile([P, PACK], F32, name="nmax", tag="nmax")
-            for u in range(2):
-                nc.vector.tensor_reduce(
-                    out=nmax[k][:, 2 * u : 2 * u + 2], in_=zb[k][u][:], axis=AX.X, op=ALU.max, negate=True
-                )
+        def row_max(k, u):
+            if u == 0:
+                nmax[k] = work.tile([P, PACK], F32, name="nmax", tag="nmax")
+            nc.vector.tensor_reduce(
+                out=nmax[k][:, 2 * u : 2 * u + 2], in_=zb[k][u][:], axis=AX.X, op=ALU.max, negate=True
+            )
 
         def exps(k):
             ex[k] = work.tile([P, PACK, E], F32, name="ex", tag="ex", align_bytes=64)
@@ -184,13 +184,18 @@ def tile_router_balance_adapter_gradient_k4_kernel(
                     out=junk[:], in0=ex[k][:, t, :], scalar=-1.0, in1=f_ps[:], op0=ALU.mult, op1=ALU.mult,
                     accum_out=ns1[:, t : t + 1],
                 )
-            eng = nc.gpsimd if k + 1 < NG else nc.vector
-            eng.tensor_tensor(out=alpha[:], in0=tok[:, :, k], in1=rinv[:], op=ALU.mult)
-            eng.tensor_tensor(out=nmean[:], in0=ns1[:], in1=rinv[:], op=ALU.mult)
-            if k + 1 == NG:
+            nc.vector.tensor_tensor(out=alpha[:], in0=tok[:, :, k], in1=rinv[:], op=ALU.mult)
+            if k + 1 < NG:
+                router(k + 1)
+                row_max(k + 1, 0)
+            else:
                 quant_dz(k - 1)
+            nc.vector.tensor_tensor(out=nmean[:], in0=ns1[:], in1=rinv[:], op=ALU.mult)
+            if k + 1 < NG:
+                row_max(k + 1, 1)
+                exps(k + 1)
             for t in range(PACK):
-                eng.tensor_scalar(
+                nc.vector.tensor_scalar(
                     out=gt[k][:, t, :], in0=f_sb[:], scalar1=nmean[:, t : t + 1], scalar2=alpha[:, t : t + 1],
                     op0=ALU.add, op1=ALU.mult,
                 )
@@ -271,7 +276,8 @@ def tile_router_balance_adapter_gradient_k4_kernel(
             in_=small[:].rearrange("p (q t r) -> p t q r", t=PACK, r=8),
         )
         quant_a(1)
-        row_max(0)
+        row_max(0, 0)
+        row_max(0, 1)
         f_ps = psum.tile([P, E], F32, name="f_ps", tag="f")
         nc.tensor.matmul(
             f_ps[:], lhsT=ident[:, LOADS_ROW : LOADS_ROW + 1].to_broadcast([P, P]), rhs=small[:, 0:E],
@@ -290,10 +296,6 @@ def tile_router_balance_adapter_gradient_k4_kernel(
         gaccs = []
         for k in range(NG):
             jacobian(k, f_ps)
-            if k + 1 < NG:
-                router(k + 1)
-                row_max(k + 1)
-                exps(k + 1)
             if k == 0:
                 perm_scales(1)
             if k + 2 < NG:

@@ -21,10 +21,11 @@ PACK = 4
 KP = P * PACK
 NG = T // KP
 DG = D // KP
-EARLY = 2
-CV = 32
-CV_LAST = 256
-A_SCALAR = 48
+EARLY = 3
+ZB, HB = 2, 4
+FV = [4, 1, 1, 1, 1, 1, 1, 2]
+A_SCALAR = 64
+Y_SCALAR = 22
 LOADS_ROW = 16
 
 
@@ -51,10 +52,11 @@ def tile_router_balance_adapter_gradient_k4_kernel(
         small = keep.tile([P, KP], BF16, align_bytes=64)
         small_p = keep.tile([P, PACK, P], BF16, align_bytes=64)
         ident = keep.tile([P, P], BF16, align_bytes=64)
-        tok = keep.tile([P, PACK, 2 * NG], F32, align_bytes=64)
+        tok = keep.tile([P, PACK, NG], F32, align_bytes=64)
         f_sb = keep.tile([P, E], F32, align_bytes=64)
         warm = keep.tile([P, 2], F32, align_bytes=64)
-        junk = keep.tile([P, E], F32, align_bytes=64)
+        junk = keep.tile([P, PACK, E], F32, align_bytes=64)
+        stat = keep.tile([P, NG, 2, PACK], F32, align_bytes=64)
         a_codes = keep.tile([P, DG, R], I32, align_bytes=64)
         a_sc = keep.tile([P, DG, R], U8, align_bytes=64)
         acc_sb = keep.tile([P, PACK, E], BF16, align_bytes=64)
@@ -84,25 +86,35 @@ def tile_router_balance_adapter_gradient_k4_kernel(
 
         nc.vector.memset(xs_raw[0][:], 0)
         nc.vector.memset(wr_sc[:].bitcast(I32), 0)
-        nc.vector.memset(small[:], 0.0)
         nc.vector.memset(warm[:], 0.0)
+        nc.vector.memset(small[:], 0.0)
         nc.vector.memset(xs_raw[1][:], 0)
         nc.scalar.activation(out=warm[:, 1:2], in_=warm[:, 0:1], func=ACT.Exp)
-
         make_identity(nc, ident[:])
+
+        def load_wr():
+            nc.sync.dma_start(out=wr_sb[:].bitcast(I32), in_=wr_words.rearrange("g p n -> p g n").bitcast(I32))
+
+        def load_ws():
+            for r in range(4):
+                nc.sync.dma_start(out=wr_sc[r:P:32, :, :].bitcast(I32), in_=ws[r].bitcast(I32))
+
+        def load_small():
+            nc.sync.dma_start(out=small[NG : 2 * NG, :], in_=token_gate.rearrange("(k n) -> k n", k=NG))
+            nc.sync.dma_start(out=small[0:NG, :], in_=token_weight.rearrange("(k n) -> k n", k=NG))
+            nc.sync.dma_start(out=small[LOADS_ROW : LOADS_ROW + 1, 0:E], in_=loads.rearrange("(o n) -> o n", o=1))
+
         load_a(0)
         load_xs(0)
         load_x(0)
         load_a(1)
-        nc.sync.dma_start(out=wr_sb[:].bitcast(I32), in_=wr_words.rearrange("g p n -> p g n").bitcast(I32))
-        for r in range(4):
-            nc.sync.dma_start(out=wr_sc[r:P:32, :, :].bitcast(I32), in_=ws[r].bitcast(I32))
-        nc.sync.dma_start(out=small[0:NG, :], in_=token_weight.rearrange("(k n) -> k n", k=NG))
-        nc.sync.dma_start(out=small[NG : 2 * NG, :], in_=token_gate.rearrange("(k n) -> k n", k=NG))
-        nc.sync.dma_start(out=small[LOADS_ROW : LOADS_ROW + 1, 0:E], in_=loads.rearrange("(o n) -> o n", o=1))
+        load_wr()
+        load_ws()
+        load_small()
         load_x(1)
+        load_x(2)
         load_xs(1)
-        for k in range(2, NG):
+        for k in range(3, NG):
             load_x(k)
         nc.sync.dma_start(out=acc_sb[:], in_=acc.rearrange("(p t) e -> p t e", t=PACK))
         nc.sync.dma_start(out=rs_sb[:], in_=rank_scale.rearrange("(p t) -> p t", t=PACK))
@@ -113,6 +125,10 @@ def tile_router_balance_adapter_gradient_k4_kernel(
         ex = {}
         s0 = {}
         gt = {}
+        rr = {}
+        hp = {}
+        ip = {}
+        ab = {}
         hb = {}
         hint = {}
         dz = {}
@@ -124,7 +140,7 @@ def tile_router_balance_adapter_gradient_k4_kernel(
             )
 
         def perm_x(k):
-            xp[k] = work.tile([P, PACK, DG * P], I32, name="xp", tag="xp", bufs=3, align_bytes=64)
+            xp[k] = work.tile([P, PACK, DG * P], I32, name="xp", tag="xp", bufs=4, align_bytes=64)
             nc.vector.tensor_copy(
                 out=xp[k][:].rearrange("p t (c r) -> p t c r", r=8),
                 in_=x_raw[k][:].rearrange("p g (q t r) -> p t (g q) r", t=PACK, r=8),
@@ -139,7 +155,7 @@ def tile_router_balance_adapter_gradient_k4_kernel(
         def router(k):
             zb[k] = []
             for u in range(2):
-                z = psum.tile([P, 2, E], F32, name="z", tag="z", bufs=3)
+                z = psum.tile([P, 2, E], F32, name="z", tag="z", bufs=ZB)
                 zb[k].append(z)
                 for tt in range(2):
                     for h in range(E // P):
@@ -171,33 +187,36 @@ def tile_router_balance_adapter_gradient_k4_kernel(
                     bias=nmax[k][:, t : t + 1], scale=1.0, accum_out=s0[k][:, t : t + 1],
                 )
 
-        def jacobian(k, f_ps):
-            ns1 = work.tile([P, PACK], F32, name="ns1", tag="ns1")
-            rinv = work.tile([P, PACK], F32, name="rinv", tag="rinv")
-            alpha = work.tile([P, PACK], F32, name="alpha", tag="alpha")
-            nmean = work.tile([P, PACK], F32, name="nmean", tag="nmean")
-            gt[k] = work.tile([P, PACK, E], F32, name="gt", tag="gt", align_bytes=64)
+        def weighted_sums(k):
+            rr[k] = work.tile([P, 2, PACK], F32, name="rr", tag="rr")
             for t in range(PACK):
                 if t == PACK - 1:
-                    nc.vector.reciprocal(out=rinv[:], in_=s0[k][:])
+                    nc.vector.reciprocal(out=rr[k][:, 0, :], in_=s0[k][:])
                 nc.vector.scalar_tensor_tensor(
-                    out=junk[:], in0=ex[k][:, t, :], scalar=-1.0, in1=f_ps[:], op0=ALU.mult, op1=ALU.mult,
-                    accum_out=ns1[:, t : t + 1],
+                    out=junk[:, t, :], in0=ex[k][:, t, :], scalar=stat[:, k, 0, t : t + 1], in1=f_sb[:],
+                    op0=ALU.mult, op1=ALU.mult, accum_out=stat[:, k, 1, t : t + 1],
                 )
-            nc.vector.tensor_tensor(out=alpha[:], in0=tok[:, :, k], in1=rinv[:], op=ALU.mult)
-            if k + 1 < NG:
-                router(k + 1)
-                row_max(k + 1, 0)
-            else:
-                quant_dz(k - 1)
-            nc.vector.tensor_tensor(out=nmean[:], in0=ns1[:], in1=rinv[:], op=ALU.mult)
-            if k + 1 < NG:
-                row_max(k + 1, 1)
-                exps(k + 1)
-            for t in range(PACK):
+            nc.vector.scalar_tensor_tensor(
+                out=rr[k][:, 1, :], in0=rr[k][:, 0, :], scalar=-1.0, in1=rr[k][:, 0, :], op0=ALU.mult, op1=ALU.mult
+            )
+
+        def coefficients(k):
+            ab[k] = work.tile([P, 2, PACK], F32, name="ab", tag="ab")
+            nc.vector.tensor_tensor(out=ab[k][:], in0=stat[:, k, :, :], in1=rr[k][:], op=ALU.mult)
+            gt[k] = work.tile([P, PACK, E], F32, name="gt", tag="gt", align_bytes=64)
+
+        def factor_scalar(k):
+            for t in range(FV[k], PACK):
+                nc.scalar.activation(
+                    out=gt[k][:, t, :], in_=f_sb[:], func=ACT.Identity, scale=ab[k][:, 0, t : t + 1],
+                    bias=ab[k][:, 1, t : t + 1],
+                )
+
+        def factor_vector(k):
+            for t in range(FV[k]):
                 nc.vector.tensor_scalar(
-                    out=gt[k][:, t, :], in0=f_sb[:], scalar1=nmean[:, t : t + 1], scalar2=alpha[:, t : t + 1],
-                    op0=ALU.add, op1=ALU.mult,
+                    out=gt[k][:, t, :], in0=f_sb[:], scalar1=ab[k][:, 0, t : t + 1], scalar2=ab[k][:, 1, t : t + 1],
+                    op0=ALU.mult, op1=ALU.add,
                 )
 
         def make_dz(k):
@@ -210,36 +229,46 @@ def tile_router_balance_adapter_gradient_k4_kernel(
             )
 
         def adapter(k):
-            hb[k] = work.tile([P, PACK, R], BF16, name="hb", tag="hb", align_bytes=64)
+            hp[k] = []
             for t in range(PACK):
-                h = psum.tile([P, R], F32, name="h", tag="h", bufs=4)
+                h = psum.tile([P, R], F32, name="h", tag="h", bufs=HB)
+                hp[k].append(h)
                 for g in range(DG):
                     codes, scales = x_operand(k, t, g)
                     nc.tensor.matmul_mx(
                         out=h[:], lhsT=codes, lhsT_scale=scales, rhs=a_codes[:, g, :].bitcast(FP8X4),
                         rhs_scale=a_sc[:, g, :], start=(g == 0), stop=(g == DG - 1),
                     )
+
+        def gate_h(k):
+            hb[k] = work.tile([P, PACK, R], BF16, name="hb", tag="hb", align_bytes=64)
+            for t in range(PACK):
                 nc.scalar.activation(
-                    out=hb[k][:, t, :], in_=h[:], func=ACT.Copy, scale=tok[:, t, NG + k : NG + k + 1]
+                    out=hb[k][:, t, :], in_=hp[k][t][:], func=ACT.Copy, scale=tok[:, t, k : k + 1]
                 )
 
-        def h_views(k, c0, c1):
-            dst = hint[k][:, c0:c1, :].rearrange("p (c i) t -> p c t i", i=4)
-            src = hb[k][:, :, c0:c1].rearrange("p t (c i) -> p c t i", i=4)
-            return dst, src
+        def interleave_h(k):
+            ip[k] = []
+            for u in range(2):
+                bank = psum.tile([P, 2, KP], BF16, name="bank", tag="i", bufs=2)
+                ip[k].append(bank)
+                for v in range(2):
+                    c0 = (2 * u + v) * P
+                    nc.tensor.matmul(
+                        bank[:, v, :].rearrange("p (c t) -> p c t", t=PACK), lhsT=ident[:],
+                        rhs=hb[k][:, :, c0 : c0 + P].rearrange("p t c -> p c t"), start=True, stop=True,
+                    )
 
-        def interleave_h_scalar(k):
-            hint[k] = work.tile([P, R, PACK], BF16, name="hint", tag="hint", align_bytes=64)
-            dst, src = h_views(k, CV if k + 1 < NG else CV_LAST, R)
-            nc.scalar.copy(out=dst, in_=src)
-
-        def interleave_h_vector(k):
-            dst, src = h_views(k, 0, CV if k + 1 < NG else CV_LAST)
-            nc.vector.tensor_copy(out=dst, in_=src)
+        def copy_h(k):
+            hint[k] = work.tile([P, R * PACK], BF16, name="hint", tag="hint", bufs=3, align_bytes=64)
+            for u in range(2):
+                nc.scalar.copy(
+                    out=hint[k][:, 2 * KP * u : 2 * KP * (u + 1)], in_=ip[k][u][:].rearrange("p v n -> p (v n)")
+                )
 
         def quant_h(k):
             nc.vector.quantize_mx(
-                out=h_codes[k][:].bitcast(FP8X4), scales=h_sc[k][:], in_=hint[k][:].rearrange("p c t -> p (c t)")
+                out=h_codes[k][:].bitcast(FP8X4), scales=h_sc[k][:], in_=hint[k][:]
             )
 
         def quant_dz(k):
@@ -265,65 +294,99 @@ def tile_router_balance_adapter_gradient_k4_kernel(
                 rhs_scale=z_sc[k][:], start=(k == 0), stop=(k == NG - 1),
             )
 
-        group_a(0)
+        def setup_tokens():
+            nc.vector.tensor_copy(
+                out=small_p[:].rearrange("p t (q r) -> p t q r", r=8),
+                in_=small[:].rearrange("p (q t r) -> p t q r", t=PACK, r=8),
+            )
+            f_ps = psum.tile([P, E], F32, name="f_ps", tag="i", bufs=2)
+            nc.tensor.matmul(
+                f_ps[:], lhsT=ident[:, LOADS_ROW : LOADS_ROW + 1].to_broadcast([P, P]), rhs=small[:, 0:E],
+                start=True, stop=True,
+            )
+            tok_ps = psum.tile([P, PACK, P], BF16, name="tok_ps", tag="i", bufs=2)
+            for t in range(PACK):
+                nc.tensor.transpose(tok_ps[:, t, :], small_p[:, t, :], ident[:])
+            nc.scalar.copy(out=tok[:], in_=tok_ps[:, :, NG : 2 * NG])
+            nc.scalar.copy(out=stat[:, :, 0, :], in_=tok_ps[:, :, 0:NG].rearrange("p t k -> p k t"))
+            nc.scalar.copy(out=f_sb[:], in_=f_ps[:])
+
         perm_scales(0)
         perm_x(0)
-        quant_a(0)
-        group_a(1)
         router(0)
-        nc.vector.tensor_copy(
-            out=small_p[:].rearrange("p t (q r) -> p t q r", r=8),
-            in_=small[:].rearrange("p (q t r) -> p t q r", t=PACK, r=8),
-        )
+        group_a(0)
+        group_a(1)
+        quant_a(0)
+        setup_tokens()
         quant_a(1)
+        adapter(0)
         row_max(0, 0)
         row_max(0, 1)
-        f_ps = psum.tile([P, E], F32, name="f_ps", tag="f")
-        nc.tensor.matmul(
-            f_ps[:], lhsT=ident[:, LOADS_ROW : LOADS_ROW + 1].to_broadcast([P, P]), rhs=small[:, 0:E],
-            start=True, stop=True,
-        )
-        tok_ps = psum.tile([P, PACK, P], BF16, name="tok_ps", tag="h", bufs=4)
-        for t in range(PACK):
-            nc.tensor.transpose(tok_ps[:, t, :], small_p[:, t, :], ident[:])
-        nc.scalar.copy(out=tok[:], in_=tok_ps[:, :, 0 : 2 * NG])
-        nc.scalar.copy(out=f_sb[:], in_=f_ps[:])
         exps(0)
+        gate_h(0)
         perm_x(1)
-        adapter(0)
-        interleave_h_scalar(0)
+        router(1)
+        adapter(1)
+        interleave_h(0)
+        gate_h(1)
+        perm_x(2)
 
         gaccs = []
         for k in range(NG):
-            jacobian(k, f_ps)
+            last = k + 1 == NG
+            weighted_sums(k)
+            if not last:
+                row_max(k + 1, 0)
+            else:
+                quant_dz(k - 1)
+            coefficients(k)
+            if not last:
+                row_max(k + 1, 1)
+            else:
+                quant_h(k)
+            factor_scalar(k)
+            factor_vector(k)
+            if not last:
+                exps(k + 1)
+                if k == 0:
+                    copy_h(0)
+                    adapter(2)
+                    router(2)
+                    interleave_h(1)
+                    gate_h(2)
+                    copy_h(1)
+                else:
+                    interleave_h(k + 1)
+                    copy_h(k + 1)
+                    if k + 2 < NG:
+                        adapter(k + 2)
+                        router(k + 2)
+                        gate_h(k + 2)
             if k == 0:
                 perm_scales(1)
-            if k + 2 < NG:
-                perm_x(k + 2)
-            if k + 1 < NG:
-                interleave_h_vector(k)
+            if k + 3 < NG:
+                perm_x(k + 3)
+            if not last:
                 if k > 0:
                     quant_dz(k - 1)
-                quant_h(k)
-                make_dz(k)
-                adapter(k + 1)
-                interleave_h_scalar(k + 1)
+                if k == 0:
+                    make_dz(k)
+                    quant_h(k)
+                else:
+                    quant_h(k)
+                    make_dz(k)
             else:
-                for t in range(PACK):
-                    grad_pass(gaccs[t], t, k - 1)
                 make_dz(k)
-                interleave_h_vector(k)
-                quant_dz(k)
-                quant_h(k)
             if k + 2 == NG:
                 for t in range(PACK):
-                    if t < 3:
-                        gacc = psum.tile([P, E], F32, name="gz", tag="z", bufs=3)
-                    else:
-                        gacc = psum.tile([P, E], F32, name="gh", tag="h", bufs=4)
+                    gacc = psum.tile([P, E], F32, name="gh", tag="h", bufs=HB)
                     gaccs.append(gacc)
                     for kk in range(NG - 2):
                         grad_pass(gacc, t, kk)
+            if last:
+                for t in range(PACK):
+                    grad_pass(gaccs[t], t, k - 1)
+                quant_dz(k)
 
         y = keep.tile([P, PACK, E], F32, align_bytes=64)
         yb = keep.tile([P, E, PACK], BF16, align_bytes=64)
@@ -337,9 +400,10 @@ def tile_router_balance_adapter_gradient_k4_kernel(
                 op0=ALU.mult, op1=ALU.add,
             )
         nc.sync.dma_start(out=out_0.rearrange("(p t) e -> p t e", t=PACK), in_=y[:])
-        nc.vector.tensor_copy(
-            out=yb[:].rearrange("p (c i) t -> p c t i", i=4), in_=y[:].rearrange("p t (c i) -> p c t i", i=4)
-        )
+        yb_v = yb[:].rearrange("p (c i) t -> p c t i", i=4)
+        y_v = y[:].rearrange("p t (c i) -> p c t i", i=4)
+        nc.scalar.copy(out=yb_v[:, :Y_SCALAR], in_=y_v[:, :Y_SCALAR])
+        nc.vector.tensor_copy(out=yb_v[:, Y_SCALAR:], in_=y_v[:, Y_SCALAR:])
         nc.vector.quantize_mx(out=y_codes[:].bitcast(FP8X4), scales=y_sc[:], in_=yb[:].rearrange("p c t -> p (c t)"))
         nc.sync.dma_start(out=out_1[0].rearrange("p m t -> p (m t)").bitcast(I32), in_=y_codes[:])
         for q in range(4):

@@ -21,9 +21,10 @@ PACK = 4
 KP = P * PACK
 NG = T // KP
 DG = D // KP
-EARLY = 3
-ZB, HB = 2, 4
-FV = [4, 1, 1, 1, 1, 1, 1, 2]
+EARLY = 2
+EXP_ORDER = (1, 0, 3, 2)
+FV = [4, 2, 1, 2, 1, 2, 1, 2]
+H_EARLY = 3
 A_SCALAR = 64
 Y_SCALAR = 22
 LOADS_ROW = 16
@@ -36,7 +37,7 @@ def tile_router_balance_adapter_gradient_k4_kernel(
     nc = tc.nc
     with ExitStack() as ctx:
         keep = ctx.enter_context(tc.tile_pool(name="keep", bufs=1))
-        work = ctx.enter_context(tc.tile_pool(name="work", bufs=2))
+        work = ctx.enter_context(tc.tile_pool(name="work", bufs=3))
         psum = ctx.enter_context(tc.psum_pool(name="psum", bufs=1))
         ctx.enter_context(tc.manual_schedule())
 
@@ -106,11 +107,11 @@ def tile_router_balance_adapter_gradient_k4_kernel(
 
         load_a(0)
         load_xs(0)
-        load_x(0)
         load_a(1)
+        load_small()
+        load_x(0)
         load_wr()
         load_ws()
-        load_small()
         load_x(1)
         load_x(2)
         load_xs(1)
@@ -140,7 +141,7 @@ def tile_router_balance_adapter_gradient_k4_kernel(
             )
 
         def perm_x(k):
-            xp[k] = work.tile([P, PACK, DG * P], I32, name="xp", tag="xp", bufs=4, align_bytes=64)
+            xp[k] = work.tile([P, PACK, DG * P], I32, name="xp", tag="xp", bufs=8, align_bytes=64)
             nc.vector.tensor_copy(
                 out=xp[k][:].rearrange("p t (c r) -> p t c r", r=8),
                 in_=x_raw[k][:].rearrange("p g (q t r) -> p t (g q) r", t=PACK, r=8),
@@ -153,10 +154,10 @@ def tile_router_balance_adapter_gradient_k4_kernel(
             return xp[k][:, t, P * g : P * (g + 1)].bitcast(FP8X4), xs_perm[ci][:, t, w0 : w0 + P // 4].bitcast(U8)
 
         def router(k):
-            zb[k] = []
-            for u in range(2):
-                z = psum.tile([P, 2, E], F32, name="z", tag="z", bufs=ZB)
-                zb[k].append(z)
+            zb[k] = {}
+            for u in (1, 0):
+                z = psum.tile([P, 2, E], F32, name="z", tag="z%d" % u)
+                zb[k][u] = z
                 for tt in range(2):
                     for h in range(E // P):
                         for g in range(DG):
@@ -172,7 +173,7 @@ def tile_router_balance_adapter_gradient_k4_kernel(
                             )
 
         def row_max(k, u):
-            if u == 0:
+            if k not in nmax:
                 nmax[k] = work.tile([P, PACK], F32, name="nmax", tag="nmax")
             nc.vector.tensor_reduce(
                 out=nmax[k][:, 2 * u : 2 * u + 2], in_=zb[k][u][:], axis=AX.X, op=ALU.max, negate=True
@@ -181,7 +182,7 @@ def tile_router_balance_adapter_gradient_k4_kernel(
         def exps(k):
             ex[k] = work.tile([P, PACK, E], F32, name="ex", tag="ex", align_bytes=64)
             s0[k] = work.tile([P, PACK], F32, name="s0", tag="s0")
-            for t in range(PACK):
+            for t in EXP_ORDER:
                 nc.scalar.activation(
                     out=ex[k][:, t, :], in_=zb[k][t // 2][:, t % 2, :], func=ACT.Exp,
                     bias=nmax[k][:, t : t + 1], scale=1.0, accum_out=s0[k][:, t : t + 1],
@@ -189,8 +190,8 @@ def tile_router_balance_adapter_gradient_k4_kernel(
 
         def weighted_sums(k):
             rr[k] = work.tile([P, 2, PACK], F32, name="rr", tag="rr")
-            for t in range(PACK):
-                if t == PACK - 1:
+            for t in (reversed(EXP_ORDER) if k > 0 else EXP_ORDER):
+                if t == (EXP_ORDER[0] if k > 0 else EXP_ORDER[-1]):
                     nc.vector.reciprocal(out=rr[k][:, 0, :], in_=s0[k][:])
                 nc.vector.scalar_tensor_tensor(
                     out=junk[:, t, :], in0=ex[k][:, t, :], scalar=stat[:, k, 0, t : t + 1], in1=f_sb[:],
@@ -228,11 +229,13 @@ def tile_router_balance_adapter_gradient_k4_kernel(
                 op=ALU.mult,
             )
 
-        def adapter(k):
-            hp[k] = []
-            for t in range(PACK):
-                h = psum.tile([P, R], F32, name="h", tag="h", bufs=HB)
-                hp[k].append(h)
+        def slot_order(k):
+            return list(range(PACK))
+
+        def adapter(k, first, last):
+            for t in slot_order(k)[first:last]:
+                h = psum.tile([P, R], F32, name="h", tag="h%d" % t)
+                hp[k, t] = h
                 for g in range(DG):
                     codes, scales = x_operand(k, t, g)
                     nc.tensor.matmul_mx(
@@ -242,29 +245,37 @@ def tile_router_balance_adapter_gradient_k4_kernel(
 
         def gate_h(k):
             hb[k] = work.tile([P, PACK, R], BF16, name="hb", tag="hb", align_bytes=64)
-            for t in range(PACK):
+            for t in slot_order(k + 1) if k > 0 else slot_order(k):
                 nc.scalar.activation(
-                    out=hb[k][:, t, :], in_=hp[k][t][:], func=ACT.Copy, scale=tok[:, t, k : k + 1]
+                    out=hb[k][:, t, :], in_=hp[k, t][:], func=ACT.Copy, scale=tok[:, t, k : k + 1]
                 )
 
         def interleave_h(k):
-            ip[k] = []
             for u in range(2):
-                bank = psum.tile([P, 2, KP], BF16, name="bank", tag="i", bufs=2)
-                ip[k].append(bank)
+                bank = psum.tile([P, E, PACK], BF16, name="bank", tag="i", bufs=2)
+                ip[k, u] = bank
                 for v in range(2):
-                    c0 = (2 * u + v) * P
                     nc.tensor.matmul(
-                        bank[:, v, :].rearrange("p (c t) -> p c t", t=PACK), lhsT=ident[:],
-                        rhs=hb[k][:, :, c0 : c0 + P].rearrange("p t c -> p c t"), start=True, stop=True,
+                        bank[:, :, 2 * v : 2 * v + 2], lhsT=ident[:],
+                        rhs=hb[k][:, 2 * v : 2 * v + 2, E * u : E * (u + 1)].rearrange("p t c -> p c t"),
+                        start=True, stop=True,
                     )
 
         def copy_h(k):
             hint[k] = work.tile([P, R * PACK], BF16, name="hint", tag="hint", bufs=3, align_bytes=64)
-            for u in range(2):
+            for u in (1, 0):
                 nc.scalar.copy(
-                    out=hint[k][:, 2 * KP * u : 2 * KP * (u + 1)], in_=ip[k][u][:].rearrange("p v n -> p (v n)")
+                    out=hint[k][:, 2 * KP * u : 2 * KP * (u + 1)], in_=ip[k, u][:].rearrange("p v n -> p (v n)")
                 )
+
+        def interleave_direct(k):
+            hint[k] = work.tile([P, R * PACK], BF16, name="hint", tag="hint", bufs=3, align_bytes=64)
+            dst = hint[k][:].rearrange("p (c i t) -> p c t i", i=4, t=PACK)
+            src = hb[k][:].rearrange("p t (c i) -> p c t i", i=4)
+            if k == 0:
+                nc.vector.tensor_copy(out=dst, in_=src)
+            else:
+                nc.scalar.copy(out=dst, in_=src)
 
         def quant_h(k):
             nc.vector.quantize_mx(
@@ -276,10 +287,17 @@ def tile_router_balance_adapter_gradient_k4_kernel(
                 out=z_codes[k][:].bitcast(FP8X4), scales=z_sc[k][:], in_=dz[k][:].rearrange("p c t -> p (c t)")
             )
 
-        def group_a(g):
+        def a_views(g):
             dst = a_grp[g][:].rearrange("p (t m) j -> p m t j", t=PACK)
             src = a_raw[g][:].rearrange("p j (m t) -> p m t j", t=PACK)
+            return dst, src
+
+        def group_a_scalar(g):
+            dst, src = a_views(g)
             nc.scalar.copy(out=dst[:, :A_SCALAR], in_=src[:, :A_SCALAR])
+
+        def group_a_vector(g):
+            dst, src = a_views(g)
             nc.vector.tensor_copy(out=dst[:, A_SCALAR:], in_=src[:, A_SCALAR:])
 
         def quant_a(g):
@@ -294,99 +312,107 @@ def tile_router_balance_adapter_gradient_k4_kernel(
                 rhs_scale=z_sc[k][:], start=(k == 0), stop=(k == NG - 1),
             )
 
-        def setup_tokens():
+        def order_tokens():
             nc.vector.tensor_copy(
                 out=small_p[:].rearrange("p t (q r) -> p t q r", r=8),
                 in_=small[:].rearrange("p (q t r) -> p t q r", t=PACK, r=8),
             )
+
+        def spread_loads():
             f_ps = psum.tile([P, E], F32, name="f_ps", tag="i", bufs=2)
             nc.tensor.matmul(
                 f_ps[:], lhsT=ident[:, LOADS_ROW : LOADS_ROW + 1].to_broadcast([P, P]), rhs=small[:, 0:E],
                 start=True, stop=True,
             )
+            nc.scalar.copy(out=f_sb[:], in_=f_ps[:])
+
+        def turn_tokens():
             tok_ps = psum.tile([P, PACK, P], BF16, name="tok_ps", tag="i", bufs=2)
             for t in range(PACK):
                 nc.tensor.transpose(tok_ps[:, t, :], small_p[:, t, :], ident[:])
             nc.scalar.copy(out=tok[:], in_=tok_ps[:, :, NG : 2 * NG])
             nc.scalar.copy(out=stat[:, :, 0, :], in_=tok_ps[:, :, 0:NG].rearrange("p t k -> p k t"))
-            nc.scalar.copy(out=f_sb[:], in_=f_ps[:])
 
+        group_a_scalar(0)
+        group_a_vector(0)
         perm_scales(0)
+        group_a_scalar(1)
+        group_a_vector(1)
+        order_tokens()
+        spread_loads()
+        turn_tokens()
         perm_x(0)
         router(0)
-        group_a(0)
-        group_a(1)
         quant_a(0)
-        setup_tokens()
         quant_a(1)
-        adapter(0)
-        row_max(0, 0)
+        adapter(0, 0, PACK)
         row_max(0, 1)
-        exps(0)
+        row_max(0, 0)
         gate_h(0)
         perm_x(1)
+        exps(0)
+        adapter(1, 0, PACK)
         router(1)
-        adapter(1)
-        interleave_h(0)
-        gate_h(1)
         perm_x(2)
+        perm_scales(1)
+        weighted_sums(0)
+        gate_h(1)
+        row_max(1, 1)
+        coefficients(0)
+        row_max(1, 0)
+        adapter(2, 0, PACK)
+        exps(1)
+        interleave_h(1)
+        factor_vector(0)
+        interleave_direct(0)
+        perm_x(3)
+        quant_h(0)
+        weighted_sums(1)
+        gate_h(2)
 
         gaccs = []
-        for k in range(NG):
-            last = k + 1 == NG
-            weighted_sums(k)
-            if not last:
-                row_max(k + 1, 0)
-            else:
-                quant_dz(k - 1)
+        for k in range(1, NG):
             coefficients(k)
-            if not last:
+            if k > 0:
+                factor_scalar(k - 1)
+            if k + 1 < NG:
+                router(k + 1)
+            if k + 1 < NG:
+                copy_h(k)
+            if k + 2 < NG:
+                adapter(k + 2, 0, PACK)
+            if k + 1 < NG:
+                row_max(k + 1, 0)
                 row_max(k + 1, 1)
             else:
+                factor_scalar(k)
+                interleave_direct(k)
+            if k + 1 < NG:
                 quant_h(k)
-            factor_scalar(k)
+            make_dz(k - 1)
             factor_vector(k)
-            if not last:
+            if k + 1 < NG:
                 exps(k + 1)
-                if k == 0:
-                    copy_h(0)
-                    adapter(2)
-                    router(2)
-                    interleave_h(1)
-                    gate_h(2)
-                    copy_h(1)
-                else:
+                if k + 2 < NG:
                     interleave_h(k + 1)
-                    copy_h(k + 1)
-                    if k + 2 < NG:
-                        adapter(k + 2)
-                        router(k + 2)
-                        gate_h(k + 2)
-            if k == 0:
-                perm_scales(1)
+                weighted_sums(k + 1)
+            if k > 0:
+                quant_dz(k - 1)
+            if k + 2 < NG:
+                gate_h(k + 2)
             if k + 3 < NG:
                 perm_x(k + 3)
-            if not last:
-                if k > 0:
-                    quant_dz(k - 1)
-                if k == 0:
-                    make_dz(k)
-                    quant_h(k)
-                else:
-                    quant_h(k)
-                    make_dz(k)
-            else:
-                make_dz(k)
             if k + 2 == NG:
                 for t in range(PACK):
-                    gacc = psum.tile([P, E], F32, name="gh", tag="h", bufs=HB)
+                    gacc = psum.tile([P, E], F32, name="gh", tag="h%d" % t)
                     gaccs.append(gacc)
                     for kk in range(NG - 2):
                         grad_pass(gacc, t, kk)
-            if last:
-                for t in range(PACK):
-                    grad_pass(gaccs[t], t, k - 1)
-                quant_dz(k)
+        make_dz(NG - 1)
+        for t in range(PACK):
+            grad_pass(gaccs[t], t, NG - 2)
+        quant_h(NG - 1)
+        quant_dz(NG - 1)
 
         y = keep.tile([P, PACK, E], F32, align_bytes=64)
         yb = keep.tile([P, E, PACK], BF16, align_bytes=64)
@@ -407,6 +433,6 @@ def tile_router_balance_adapter_gradient_k4_kernel(
         nc.vector.quantize_mx(out=y_codes[:].bitcast(FP8X4), scales=y_sc[:], in_=yb[:].rearrange("p c t -> p (c t)"))
         nc.sync.dma_start(out=out_1[0].rearrange("p m t -> p (m t)").bitcast(I32), in_=y_codes[:])
         for q in range(4):
-            nc.sync.dma_start(
+            (nc.sync if q % 2 else nc.scalar).dma_start(
                 out=out_2[0][4 * q : 4 * q + 4, :].bitcast(I32), in_=y_sc[32 * q : 32 * q + 4, :].bitcast(I32)
             )

@@ -23,11 +23,12 @@ NG = T // KP
 DG = D // KP
 EARLY = 2
 EXP_ORDER = (1, 0, 3, 2)
-FV = [4, 2, 1, 2, 1, 2, 1, 2]
+FV = [4, 2, 2, 3, 3, 2, 1, 1]
 H_EARLY = 3
 A_SCALAR = 64
 Y_SCALAR = 22
 LOADS_ROW = 16
+DMA_ORDERED = 2
 
 
 def tile_router_balance_adapter_gradient_k4_kernel(
@@ -62,7 +63,7 @@ def tile_router_balance_adapter_gradient_k4_kernel(
         a_sc = keep.tile([P, DG, R], U8, align_bytes=64)
         acc_sb = keep.tile([P, PACK, E], BF16, align_bytes=64)
         rs_sb = keep.tile([P, PACK], BF16, align_bytes=64)
-        x_raw = [keep.tile([P, DG, KP], I32, name="x_raw%d" % k, align_bytes=64) for k in range(NG)]
+        x_raw = [keep.tile([P, DG, KP], I32, name="x_raw%d" % k, align_bytes=64) for k in range(NG - DMA_ORDERED)]
         a_raw = [keep.tile([P, PACK, R], BF16, name="a_raw%d" % g, align_bytes=64) for g in range(DG)]
         a_grp = [keep.tile([P, R, PACK], BF16, name="a_grp%d" % g, align_bytes=64) for g in range(DG)]
         h_codes = [keep.tile([P, R], I32, name="h_codes%d" % k, align_bytes=64) for k in range(NG)]
@@ -76,6 +77,15 @@ def tile_router_balance_adapter_gradient_k4_kernel(
 
         def load_x(k):
             nc.sync.dma_start(out=x_raw[k][:], in_=xw[:, :, 4 * KP * k : 4 * KP * (k + 1)].bitcast(I32))
+
+        def load_x_ordered(k):
+            xp[k] = keep.tile([P, PACK, DG * P], I32, name="xp%d" % k, align_bytes=64)
+            words = xw[:, :, 4 * KP * k : 4 * KP * (k + 1)].bitcast(I32).rearrange("p g (q t r) -> g t p q r", t=PACK, r=8)
+            for t in range(PACK):
+                for g in range(DG):
+                    nc.sync.dma_start(
+                        out=xp[k][:, t, P * g : P * (g + 1)].rearrange("p (q r) -> p q r", r=8), in_=words[g, t]
+                    )
 
         def load_xs(ci):
             g0, g1 = chunks[ci]
@@ -115,12 +125,14 @@ def tile_router_balance_adapter_gradient_k4_kernel(
         load_x(1)
         load_x(2)
         load_xs(1)
-        for k in range(3, NG):
+        for k in range(3, NG - DMA_ORDERED):
             load_x(k)
-        nc.sync.dma_start(out=acc_sb[:], in_=acc.rearrange("(p t) e -> p t e", t=PACK))
-        nc.sync.dma_start(out=rs_sb[:], in_=rank_scale.rearrange("(p t) -> p t", t=PACK))
 
         xp = {}
+        for k in range(NG - DMA_ORDERED, NG):
+            load_x_ordered(k)
+        nc.sync.dma_start(out=acc_sb[:], in_=acc.rearrange("(p t) e -> p t e", t=PACK))
+        nc.sync.dma_start(out=rs_sb[:], in_=rank_scale.rearrange("(p t) -> p t", t=PACK))
         zb = {}
         nmax = {}
         ex = {}
@@ -377,8 +389,7 @@ def tile_router_balance_adapter_gradient_k4_kernel(
                 factor_scalar(k - 1)
             if k + 1 < NG:
                 router(k + 1)
-            if k + 1 < NG:
-                copy_h(k)
+            copy_h(k)
             if k + 2 < NG:
                 adapter(k + 2, 0, PACK)
             if k + 1 < NG:
@@ -386,21 +397,18 @@ def tile_router_balance_adapter_gradient_k4_kernel(
                 row_max(k + 1, 1)
             else:
                 factor_scalar(k)
-                interleave_direct(k)
-            if k + 1 < NG:
-                quant_h(k)
+            quant_h(k)
             make_dz(k - 1)
             factor_vector(k)
             if k + 1 < NG:
                 exps(k + 1)
-                if k + 2 < NG:
-                    interleave_h(k + 1)
+                interleave_h(k + 1)
                 weighted_sums(k + 1)
             if k > 0:
                 quant_dz(k - 1)
             if k + 2 < NG:
                 gate_h(k + 2)
-            if k + 3 < NG:
+            if k + 3 < NG - DMA_ORDERED:
                 perm_x(k + 3)
             if k + 2 == NG:
                 for t in range(PACK):
@@ -411,7 +419,6 @@ def tile_router_balance_adapter_gradient_k4_kernel(
         make_dz(NG - 1)
         for t in range(PACK):
             grad_pass(gaccs[t], t, NG - 2)
-        quant_h(NG - 1)
         quant_dz(NG - 1)
 
         y = keep.tile([P, PACK, E], F32, align_bytes=64)

from contextlib import ExitStack

import concourse.mybir as mybir
from concourse.masks import make_identity

T, D, R, E = 4096, 1024, 512, 256
FLOPS = 2 * T * D * (R + E) + 2 * T * R * E

F32 = mybir.dt.float32
BF16 = mybir.dt.bfloat16
I32 = mybir.dt.int32
U8 = mybir.dt.uint8
FP8X4 = mybir.dt.float8_e4m3fn_x4
FP4X4 = mybir.dt.float4_e2m1fn_x4
ALU = mybir.AluOpType
ACT = mybir.ActivationFunctionType
AX = mybir.AxisListType

P = 128
PACK = 4
KP = P * PACK
NG = T // KP
DG = D // KP
EARLY = 2
EXP_ORDER = (1, 0, 3, 2)
FV = [4, 2, 2, 3, 3, 2, 1, 1]
H_EARLY = 3
A_SCALAR = 64
Y_SCALAR = 22
LOADS_ROW = 16
DMA_ORDERED = 2


def tile_router_balance_adapter_gradient_k4_kernel(
    tc, x_words, x_scales, wr_words, wr_scales, a, loads, token_weight, token_gate, rank_scale, acc,
    out_0, out_1, out_2,
):
    nc = tc.nc
    with ExitStack() as ctx:
        keep = ctx.enter_context(tc.tile_pool(name="keep", bufs=1))
        work = ctx.enter_context(tc.tile_pool(name="work", bufs=3))
        psum = ctx.enter_context(tc.psum_pool(name="psum", bufs=1))
        ctx.enter_context(tc.manual_schedule())

        chunks = [(0, EARLY), (EARLY, NG)]
        xs_raw = []
        xs_perm = []
        for ci, (g0, g1) in enumerate(chunks):
            n = g1 - g0
            xs_raw.append(keep.tile([P, DG, n * KP // 4], I32, name="xs_raw%d" % ci, align_bytes=64))
            xs_perm.append(keep.tile([P, PACK, DG * n * P // 4], I32, name="xs_perm%d" % ci, align_bytes=64))
        wr_sb = keep.tile([P, DG, 2 * E], U8, align_bytes=64)
        wr_sc = keep.tile([P, DG, E], U8, align_bytes=64)
        small = keep.tile([P, KP], BF16, align_bytes=64)
        small_p = keep.tile([P, PACK, P], BF16, align_bytes=64)
        ident = keep.tile([P, P], BF16, align_bytes=64)
        tok = keep.tile([P, PACK, NG], F32, align_bytes=64)
        f_sb = keep.tile([P, E], F32, align_bytes=64)
        warm = keep.tile([P, 2], F32, align_bytes=64)
        junk = keep.tile([P, PACK, E], F32, align_bytes=64)
        stat = keep.tile([P, NG, 2, PACK], F32, align_bytes=64)
        a_codes = keep.tile([P, DG, R], I32, align_bytes=64)
        a_sc = keep.tile([P, DG, R], U8, align_bytes=64)
        acc_sb = keep.tile([P, PACK, E], BF16, align_bytes=64)
        rs_sb = keep.tile([P, PACK], BF16, align_bytes=64)
        x_raw = [keep.tile([P, DG, KP], I32, name="x_raw%d" % k, align_bytes=64) for k in range(NG - DMA_ORDERED)]
        a_raw = [keep.tile([P, PACK, R], BF16, name="a_raw%d" % g, align_bytes=64) for g in range(DG)]
        a_grp = [keep.tile([P, R, PACK], BF16, name="a_grp%d" % g, align_bytes=64) for g in range(DG)]
        h_codes = [keep.tile([P, R], I32, name="h_codes%d" % k, align_bytes=64) for k in range(NG)]
        h_sc = [keep.tile([P, R], U8, name="h_sc%d" % k, align_bytes=64) for k in range(NG)]
        z_codes = [keep.tile([P, E], I32, name="z_codes%d" % k, align_bytes=64) for k in range(NG)]
        z_sc = [keep.tile([P, E], U8, name="z_sc%d" % k, align_bytes=64) for k in range(NG)]

        xw = x_words.rearrange("g p n t -> p g (n t)")
        xs = x_scales.rearrange("g (q r) n -> r q g n", r=4)
        ws = wr_scales.rearrange("g (q r) n -> r q g n", r=4)

        def load_x(k):
            nc.sync.dma_start(out=x_raw[k][:], in_=xw[:, :, 4 * KP * k : 4 * KP * (k + 1)].bitcast(I32))

        def load_x_ordered(k):
            xp[k] = keep.tile([P, PACK, DG * P], I32, name="xp%d" % k, align_bytes=64)
            words = xw[:, :, 4 * KP * k : 4 * KP * (k + 1)].bitcast(I32).rearrange("p g (q t r) -> g t p q r", t=PACK, r=8)
            for t in range(PACK):
                for g in range(DG):
                    nc.sync.dma_start(
                        out=xp[k][:, t, P * g : P * (g + 1)].rearrange("p (q r) -> p q r", r=8), in_=words[g, t]
                    )

        def load_xs(ci):
            g0, g1 = chunks[ci]
            for r in range(4):
                nc.sync.dma_start(out=xs_raw[ci][r:P:32, :, :], in_=xs[r][:, :, KP * g0 : KP * g1].bitcast(I32))

        def load_a(g):
            nc.sync.dma_start(out=a_raw[g][:], in_=a[KP * g : KP * (g + 1), :].rearrange("(p j) c -> p j c", j=PACK))

        nc.vector.memset(xs_raw[0][:], 0)
        nc.vector.memset(wr_sc[:].bitcast(I32), 0)
        nc.vector.memset(warm[:], 0.0)
        nc.vector.memset(small[:], 0.0)
        nc.vector.memset(xs_raw[1][:], 0)
        nc.scalar.activation(out=warm[:, 1:2], in_=warm[:, 0:1], func=ACT.Exp)
        make_identity(nc, ident[:])

        def load_wr():
            nc.sync.dma_start(out=wr_sb[:].bitcast(I32), in_=wr_words.rearrange("g p n -> p g n").bitcast(I32))

        def load_ws():
            for r in range(4):
                nc.sync.dma_start(out=wr_sc[r:P:32, :, :].bitcast(I32), in_=ws[r].bitcast(I32))

        def load_small():
            nc.sync.dma_start(out=small[NG : 2 * NG, :], in_=token_gate.rearrange("(k n) -> k n", k=NG))
            nc.sync.dma_start(out=small[0:NG, :], in_=token_weight.rearrange("(k n) -> k n", k=NG))
            nc.sync.dma_start(out=small[LOADS_ROW : LOADS_ROW + 1, 0:E], in_=loads.rearrange("(o n) -> o n", o=1))

        load_a(0)
        load_xs(0)
        load_a(1)
        load_small()
        load_x(0)
        load_wr()
        load_ws()
        load_x(1)
        load_x(2)
        load_xs(1)
        for k in range(3, NG - DMA_ORDERED):
            load_x(k)

        xp = {}
        for k in range(NG - DMA_ORDERED, NG):
            load_x_ordered(k)
        nc.sync.dma_start(out=acc_sb[:], in_=acc.rearrange("(p t) e -> p t e", t=PACK))
        nc.sync.dma_start(out=rs_sb[:], in_=rank_scale.rearrange("(p t) -> p t", t=PACK))
        zb = {}
        nmax = {}
        ex = {}
        s0 = {}
        gt = {}
        rr = {}
        hp = {}
        ip = {}
        ab = {}
        hb = {}
        hint = {}
        dz = {}

        def perm_scales(ci):
            nc.vector.tensor_copy(
                out=xs_perm[ci][:].rearrange("p t (c r) -> p t c r", r=2),
                in_=xs_raw[ci][:].rearrange("p g (c t r) -> p t (g c) r", t=PACK, r=2),
            )

        def perm_x(k):
            xp[k] = work.tile([P, PACK, DG * P], I32, name="xp", tag="xp", bufs=8, align_bytes=64)
            nc.vector.tensor_copy(
                out=xp[k][:].rearrange("p t (c r) -> p t c r", r=8),
                in_=x_raw[k][:].rearrange("p g (q t r) -> p t (g q) r", t=PACK, r=8),
            )

        def x_operand(k, t, g):
            ci = 0 if k < EARLY else 1
            g0, g1 = chunks[ci]
            w0 = (g * (g1 - g0) + k - g0) * (P // 4)
            return xp[k][:, t, P * g : P * (g + 1)].bitcast(FP8X4), xs_perm[ci][:, t, w0 : w0 + P // 4].bitcast(U8)

        def router(k):
            zb[k] = {}
            for u in (1, 0):
                z = psum.tile([P, 2, E], F32, name="z", tag="z%d" % u)
                zb[k][u] = z
                for tt in range(2):
                    for h in range(E // P):
                        for g in range(DG):
                            codes, scales = x_operand(k, 2 * u + tt, g)
                            nc.tensor.matmul_mx(
                                out=z[:, tt, P * h : P * (h + 1)],
                                lhsT=codes,
                                lhsT_scale=scales,
                                rhs=wr_sb[:, g, 2 * P * h : 2 * P * (h + 1)].bitcast(FP4X4),
                                rhs_scale=wr_sc[:, g, P * h : P * (h + 1)],
                                start=(g == 0),
                                stop=(g == DG - 1),
                            )

        def row_max(k, u):
            if k not in nmax:
                nmax[k] = work.tile([P, PACK], F32, name="nmax", tag="nmax")
            nc.vector.tensor_reduce(
                out=nmax[k][:, 2 * u : 2 * u + 2], in_=zb[k][u][:], axis=AX.X, op=ALU.max, negate=True
            )

        def exps(k):
            ex[k] = work.tile([P, PACK, E], F32, name="ex", tag="ex", align_bytes=64)
            s0[k] = work.tile([P, PACK], F32, name="s0", tag="s0")
            for t in EXP_ORDER:
                nc.scalar.activation(
                    out=ex[k][:, t, :], in_=zb[k][t // 2][:, t % 2, :], func=ACT.Exp,
                    bias=nmax[k][:, t : t + 1], scale=1.0, accum_out=s0[k][:, t : t + 1],
                )

        def weighted_sums(k):
            rr[k] = work.tile([P, 2, PACK], F32, name="rr", tag="rr")
            for t in (reversed(EXP_ORDER) if k > 0 else EXP_ORDER):
                if t == (EXP_ORDER[0] if k > 0 else EXP_ORDER[-1]):
                    nc.vector.reciprocal(out=rr[k][:, 0, :], in_=s0[k][:])
                nc.vector.scalar_tensor_tensor(
                    out=junk[:, t, :], in0=ex[k][:, t, :], scalar=stat[:, k, 0, t : t + 1], in1=f_sb[:],
                    op0=ALU.mult, op1=ALU.mult, accum_out=stat[:, k, 1, t : t + 1],
                )
            nc.vector.scalar_tensor_tensor(
                out=rr[k][:, 1, :], in0=rr[k][:, 0, :], scalar=-1.0, in1=rr[k][:, 0, :], op0=ALU.mult, op1=ALU.mult
            )

        def coefficients(k):
            ab[k] = work.tile([P, 2, PACK], F32, name="ab", tag="ab")
            nc.vector.tensor_tensor(out=ab[k][:], in0=stat[:, k, :, :], in1=rr[k][:], op=ALU.mult)
            gt[k] = work.tile([P, PACK, E], F32, name="gt", tag="gt", align_bytes=64)

        def factor_scalar(k):
            for t in range(FV[k], PACK):
                nc.scalar.activation(
                    out=gt[k][:, t, :], in_=f_sb[:], func=ACT.Identity, scale=ab[k][:, 0, t : t + 1],
                    bias=ab[k][:, 1, t : t + 1],
                )

        def factor_vector(k):
            for t in range(FV[k]):
                nc.vector.tensor_scalar(
                    out=gt[k][:, t, :], in0=f_sb[:], scalar1=ab[k][:, 0, t : t + 1], scalar2=ab[k][:, 1, t : t + 1],
                    op0=ALU.mult, op1=ALU.add,
                )

        def make_dz(k):
            dz[k] = work.tile([P, E, PACK], BF16, name="dz", tag="dz", align_bytes=64)
            nc.vector.tensor_tensor(
                out=dz[k][:].rearrange("p (c i) t -> p c t i", i=4),
                in0=ex[k][:].rearrange("p t (c i) -> p c t i", i=4),
                in1=gt[k][:].rearrange("p t (c i) -> p c t i", i=4),
                op=ALU.mult,
            )

        def slot_order(k):
            return list(range(PACK))

        def adapter(k, first, last):
            for t in slot_order(k)[first:last]:
                h = psum.tile([P, R], F32, name="h", tag="h%d" % t)
                hp[k, t] = h
                for g in range(DG):
                    codes, scales = x_operand(k, t, g)
                    nc.tensor.matmul_mx(
                        out=h[:], lhsT=codes, lhsT_scale=scales, rhs=a_codes[:, g, :].bitcast(FP8X4),
                        rhs_scale=a_sc[:, g, :], start=(g == 0), stop=(g == DG - 1),
                    )

        def gate_h(k):
            hb[k] = work.tile([P, PACK, R], BF16, name="hb", tag="hb", align_bytes=64)
            for t in slot_order(k + 1) if k > 0 else slot_order(k):
                nc.scalar.activation(
                    out=hb[k][:, t, :], in_=hp[k, t][:], func=ACT.Copy, scale=tok[:, t, k : k + 1]
                )

        def interleave_h(k):
            for u in range(2):
                bank = psum.tile([P, E, PACK], BF16, name="bank", tag="i", bufs=2)
                ip[k, u] = bank
                for v in range(2):
                    nc.tensor.matmul(
                        bank[:, :, 2 * v : 2 * v + 2], lhsT=ident[:],
                        rhs=hb[k][:, 2 * v : 2 * v + 2, E * u : E * (u + 1)].rearrange("p t c -> p c t"),
                        start=True, stop=True,
                    )

        def copy_h(k):
            hint[k] = work.tile([P, R * PACK], BF16, name="hint", tag="hint", bufs=3, align_bytes=64)
            for u in (1, 0):
                nc.scalar.copy(
                    out=hint[k][:, 2 * KP * u : 2 * KP * (u + 1)], in_=ip[k, u][:].rearrange("p v n -> p (v n)")
                )

        def interleave_direct(k):
            hint[k] = work.tile([P, R * PACK], BF16, name="hint", tag="hint", bufs=3, align_bytes=64)
            dst = hint[k][:].rearrange("p (c i t) -> p c t i", i=4, t=PACK)
            src = hb[k][:].rearrange("p t (c i) -> p c t i", i=4)
            if k == 0:
                nc.vector.tensor_copy(out=dst, in_=src)
            else:
                nc.scalar.copy(out=dst, in_=src)

        def quant_h(k):
            nc.vector.quantize_mx(
                out=h_codes[k][:].bitcast(FP8X4), scales=h_sc[k][:], in_=hint[k][:]
            )

        def quant_dz(k):
            nc.vector.quantize_mx(
                out=z_codes[k][:].bitcast(FP8X4), scales=z_sc[k][:], in_=dz[k][:].rearrange("p c t -> p (c t)")
            )

        def a_views(g):
            dst = a_grp[g][:].rearrange("p (t m) j -> p m t j", t=PACK)
            src = a_raw[g][:].rearrange("p j (m t) -> p m t j", t=PACK)
            return dst, src

        def group_a_scalar(g):
            dst, src = a_views(g)
            nc.scalar.copy(out=dst[:, :A_SCALAR], in_=src[:, :A_SCALAR])

        def group_a_vector(g):
            dst, src = a_views(g)
            nc.vector.tensor_copy(out=dst[:, A_SCALAR:], in_=src[:, A_SCALAR:])

        def quant_a(g):
            nc.vector.quantize_mx(
                out=a_codes[:, g, :].bitcast(FP8X4), scales=a_sc[:, g, :], in_=a_grp[g][:].rearrange("p c j -> p (c j)")
            )

        def grad_pass(gacc, t, k):
            nc.tensor.matmul_mx(
                out=gacc[:], lhsT=h_codes[k][:, P * t : P * (t + 1)].bitcast(FP8X4),
                lhsT_scale=h_sc[k][:, P * t : P * (t + 1)], rhs=z_codes[k][:].bitcast(FP8X4),
                rhs_scale=z_sc[k][:], start=(k == 0), stop=(k == NG - 1),
            )

        def order_tokens():
            nc.vector.tensor_copy(
                out=small_p[:].rearrange("p t (q r) -> p t q r", r=8),
                in_=small[:].rearrange("p (q t r) -> p t q r", t=PACK, r=8),
            )

        def spread_loads():
            f_ps = psum.tile([P, E], F32, name="f_ps", tag="i", bufs=2)
            nc.tensor.matmul(
                f_ps[:], lhsT=ident[:, LOADS_ROW : LOADS_ROW + 1].to_broadcast([P, P]), rhs=small[:, 0:E],
                start=True, stop=True,
            )
            nc.scalar.copy(out=f_sb[:], in_=f_ps[:])

        def turn_tokens():
            tok_ps = psum.tile([P, PACK, P], BF16, name="tok_ps", tag="i", bufs=2)
            for t in range(PACK):
                nc.tensor.transpose(tok_ps[:, t, :], small_p[:, t, :], ident[:])
            nc.scalar.copy(out=tok[:], in_=tok_ps[:, :, NG : 2 * NG])
            nc.scalar.copy(out=stat[:, :, 0, :], in_=tok_ps[:, :, 0:NG].rearrange("p t k -> p k t"))

        group_a_scalar(0)
        group_a_vector(0)
        perm_scales(0)
        group_a_scalar(1)
        group_a_vector(1)
        order_tokens()
        spread_loads()
        turn_tokens()
        perm_x(0)
        router(0)
        quant_a(0)
        quant_a(1)
        adapter(0, 0, PACK)
        row_max(0, 1)
        row_max(0, 0)
        gate_h(0)
        perm_x(1)
        exps(0)
        adapter(1, 0, PACK)
        router(1)
        perm_x(2)
        perm_scales(1)
        weighted_sums(0)
        gate_h(1)
        row_max(1, 1)
        coefficients(0)
        row_max(1, 0)
        adapter(2, 0, PACK)
        exps(1)
        interleave_h(1)
        factor_vector(0)
        interleave_direct(0)
        perm_x(3)
        quant_h(0)
        weighted_sums(1)
        gate_h(2)

        gaccs = []
        for k in range(1, NG):
            coefficients(k)
            if k > 0:
                factor_scalar(k - 1)
            if k + 1 < NG:
                router(k + 1)
            copy_h(k)
            if k + 2 < NG:
                adapter(k + 2, 0, PACK)
            if k + 1 < NG:
                row_max(k + 1, 0)
                row_max(k + 1, 1)
            else:
                factor_scalar(k)
            quant_h(k)
            make_dz(k - 1)
            factor_vector(k)
            if k + 1 < NG:
                exps(k + 1)
                interleave_h(k + 1)
                weighted_sums(k + 1)
            if k > 0:
                quant_dz(k - 1)
            if k + 2 < NG:
                gate_h(k + 2)
            if k + 3 < NG - DMA_ORDERED:
                perm_x(k + 3)
            if k + 2 == NG:
                for t in range(PACK):
                    gacc = psum.tile([P, E], F32, name="gh", tag="h%d" % t)
                    gaccs.append(gacc)
                    for kk in range(NG - 2):
                        grad_pass(gacc, t, kk)
        make_dz(NG - 1)
        for t in range(PACK):
            grad_pass(gaccs[t], t, NG - 2)
        quant_dz(NG - 1)

        y = keep.tile([P, PACK, E], F32, align_bytes=64)
        yb = keep.tile([P, E, PACK], BF16, align_bytes=64)
        y_codes = keep.tile([P, E], I32, align_bytes=64)
        y_sc = keep.tile([P, E], U8, align_bytes=64)
        for t in range(PACK):
            grad_pass(gaccs[t], t, NG - 1)
        for t in range(PACK):
            nc.vector.scalar_tensor_tensor(
                out=y[:, t, :], in0=gaccs[t][:], scalar=rs_sb[:, t : t + 1], in1=acc_sb[:, t, :],
                op0=ALU.mult, op1=ALU.add,
            )
        nc.sync.dma_start(out=out_0.rearrange("(p t) e -> p t e", t=PACK), in_=y[:])
        yb_v = yb[:].rearrange("p (c i) t -> p c t i", i=4)
        y_v = y[:].rearrange("p t (c i) -> p c t i", i=4)
        nc.scalar.copy(out=yb_v[:, :Y_SCALAR], in_=y_v[:, :Y_SCALAR])
        nc.vector.tensor_copy(out=yb_v[:, Y_SCALAR:], in_=y_v[:, Y_SCALAR:])
        nc.vector.quantize_mx(out=y_codes[:].bitcast(FP8X4), scales=y_sc[:], in_=yb[:].rearrange("p c t -> p (c t)"))
        nc.sync.dma_start(out=out_1[0].rearrange("p m t -> p (m t)").bitcast(I32), in_=y_codes[:])
        for q in range(4):
            (nc.sync if q % 2 else nc.scalar).dma_start(
                out=out_2[0][4 * q : 4 * q + 4, :].bitcast(I32), in_=y_sc[32 * q : 32 * q + 4, :].bitcast(I32)
            )
